import numpy as np
import ml_dtypes


def mxq(x, axis, fmt="e4m3"):
    dtype, down = {"e4m3": (ml_dtypes.float8_e4m3fn, 7), "e5m2": (ml_dtypes.float8_e5m2, 14)}[fmt]
    v = np.moveaxis(np.asarray(x, np.float32).astype(ml_dtypes.bfloat16).astype(np.float64), axis, -1)
    blocks = v.reshape(v.shape[:-1] + (-1, 32))
    amax = np.abs(blocks).max(-1, keepdims=True)
    byte = np.maximum(np.where(amax > 0, np.frexp(amax)[1] - 1 + 127, 0) - down, 1)
    scale = np.exp2(byte - 127.0)
    codes = (blocks / scale).astype(np.float32).astype(dtype).astype(np.float64)
    return np.moveaxis((codes * scale).reshape(v.shape), -1, axis)


WIDE = False


def mx_kscale(k):
    if not WIDE:
        return np.ones(k)
    levels = np.array([30, -30])
    if k % 512:
        return np.exp2(np.random.permutation(np.resize(levels, k // 32))).repeat(32)
    a = np.empty((k // 512, 16))
    for p in range(k // 512):
        a[p, :8] = np.random.permutation(np.resize(levels, 8))
        for g in range(8):
            far = levels[np.abs(levels - a[p, g]) >= 10]
            a[p, g + 8] = far[np.random.randint(len(far))]
    return np.exp2(a.ravel()).repeat(32)


def f64(x):
    return np.asarray(x).astype(np.float64)


def striped(idx):
    return np.tile(np.asarray(idx).reshape(-1, 16).T, (8, 1)).astype(np.uint16)


def unstriped(offs):
    return offs[:16].T.reshape(-1).astype(np.int64)


E2M1 = np.array([0.0, 0.5, 1.0, 1.5, 2.0, 3.0, 4.0, 6.0, -0.0, -0.5, -1.0, -1.5, -2.0, -3.0, -4.0, -6.0])


def pack_weight(w, fmt):
    k, n = w.shape
    w = f64(np.asarray(w, np.float32).astype(ml_dtypes.bfloat16)).reshape(k // 32, 32, n)
    amax = np.abs(w).max(1)
    if fmt in ("e4m3", "e5m2"):
        byte = np.frexp(amax)[1] - 1 + 127 - (7 if fmt == "e4m3" else 14)
    else:
        mant, ex = np.frexp(amax / 6.0)
        byte = np.where(mant > 0.5, ex, ex - 1) + 127
    byte = np.clip(np.where(amax > 0, byte, 1), 1, 254)
    scaled = (w * np.exp2(127.0 - byte)[:, None, :]).reshape(k, n).astype(np.float32)
    by_word = np.ascontiguousarray(scaled.reshape(k // 512, 128, 4, n).transpose(0, 1, 3, 2))
    if fmt in ("e4m3", "e5m2"):
        words = by_word.astype(ml_dtypes.float8_e4m3fn if fmt == "e4m3" else ml_dtypes.float8_e5m2).view(np.uint8)
    else:
        c = by_word.astype(ml_dtypes.float4_e2m1fn).view(np.uint8) & 0xF
        words = (c[..., 0::2] | (c[..., 1::2] << 4)).reshape(k // 512, 128, 2 * n)
    return np.ascontiguousarray(words), np.ascontiguousarray(byte.astype(np.uint8).reshape(k // 512, 16, n))


def unpack_weight(words, scales, fmt):
    g, _, n = scales.shape
    words = np.ascontiguousarray(words).reshape(g, 128, n, -1)
    if fmt in ("e4m3", "e5m2"):
        vals = words.view(ml_dtypes.float8_e4m3fn if fmt == "e4m3" else ml_dtypes.float8_e5m2).astype(np.float64)
    else:
        nib = np.empty((g, 128, n, 4), np.uint8)
        nib[..., 0::2] = words & 0xF
        nib[..., 1::2] = words >> 4
        vals = E2M1[nib]
    vals = vals * np.repeat(np.exp2(scales.astype(np.float64) - 127.0), 8, axis=1)[..., None]
    return vals.transpose(0, 1, 3, 2).reshape(g * 512, n)


K, T, J, R, F, V, N = 512, 512, 256, 512, 512, 512, 256


def setup_inputs():
    n = np.random.standard_normal
    idx = np.random.permutation(T)[:J]
    idx2 = np.random.permutation(T)[:J]
    idx3 = np.random.permutation(V)[:J]
    fk = mx_kscale(K)
    fr = mx_kscale(R)
    ff = mx_kscale(F)
    wp = pack_weight(n((K, R)) * 1 / np.sqrt(K) * fk[:, None] * fr, "e2m1")
    w2p = pack_weight(n((F, R)) * 1 / np.sqrt(F) * ff[:, None] * fr, "e5m2")
    wbp = pack_weight(n((R, N)) * 1 / np.sqrt(R) / fr[:, None], "e5m2")
    return {
        "xf": (n((K, T))).astype(np.float32),
        "fk": (np.random.uniform(0.5, 2.0, (K, 1)) / fk[:, None]).astype(np.float32),
        "w_words": wp[0],
        "w_scales": wp[1],
        "so": (n((F, J))).astype(np.float32),
        "fl": (np.random.uniform(0.5, 2.0, (F, 1)) / ff[:, None]).astype(np.float32),
        "w2_words": w2p[0],
        "w2_scales": w2p[1],
        "tb": (n((R, V)) * 0.7 * fr[:, None]).astype(np.float32),
        "wb_words": wbp[0],
        "wb_scales": wbp[1],
        "rs": (1.0 * n((J, N))).astype(np.float32),
        "offs": striped(idx),
        "offs2": striped(idx2),
        "offs3": striped(idx3),
    }


def reference(xf, fk, w_words, w_scales, so, fl, w2_words, w2_scales, tb, wb_words, wb_scales, rs, offs, offs2, offs3):
    idx = unstriped(offs)
    idx2 = unstriped(offs2)
    idx3 = unstriped(offs3)
    wu = unpack_weight(w_words, w_scales, "e2m1")
    w2u = unpack_weight(w2_words, w2_scales, "e5m2")
    wbu = unpack_weight(wb_words, wb_scales, "e5m2")
    u = (f64(xf)[:, idx] - f64(xf)[:, idx2]) * f64(fk)
    s1 = np.pad(f64(so), ((0, 0), (1, 0)))[:, :J]
    u2 = (f64(so) - 0.8 * s1) * f64(fl)
    uq = mxq(u, 0, "e4m3")
    u2q = mxq(u2, 0, "e5m2")
    a = wu.T @ uq + w2u.T @ u2q
    hid = np.maximum(a - f64(tb)[:, idx3], 0.0)
    hidq = mxq(hid, 0, "e5m2")
    p = hidq.T @ wbu
    pk2 = np.max(np.abs(p), axis=1, keepdims=True)
    y = p / (pk2 + 0.2) + 0.3 * f64(rs)
    return y

@@ -1,0 +1,199 @@
+from contextlib import ExitStack
+
+import concourse.mybir as mybir
+
+K, T, J, R, F, V, N = 512, 512, 256, 512, 512, 512, 256
+FLOPS = 2 * (K * R * J + F * R * J + R * J * N)
+
+F32 = mybir.dt.float32
+BF16 = mybir.dt.bfloat16
+I32 = mybir.dt.int32
+U32 = mybir.dt.uint32
+U16 = mybir.dt.uint16
+U8 = mybir.dt.uint8
+E4M3 = mybir.dt.float8_e4m3fn_x4
+E5M2 = mybir.dt.float8_e5m2_x4
+E2M1 = mybir.dt.float4_e2m1fn_x4
+ALU = mybir.AluOpType
+ACT = mybir.ActivationFunctionType
+
+P = 128
+PACK = 4
+HALF = 128
+HALVES = J // HALF
+LIST_COLS = HALF // 16
+PAD = 4
+
+
+def tile_list_sum_pickgaps_stepped_overtable_rowpeaks_kernel(
+    tc, xf, fk, w_words, w_scales, so, fl, w2_words, w2_scales, tb, wb_words, wb_scales, rs, offs, offs2, offs3, out
+):
+    nc = tc.nc
+    with ExitStack() as ctx:
+        keep = ctx.enter_context(tc.tile_pool(name="keep", bufs=1))
+        psum = ctx.enter_context(tc.psum_pool(name="psum", bufs=1))
+
+        def sb(name, shape, dtype):
+            return keep.tile(shape, dtype, name=name, align_bytes=64)
+
+        first = sb("first", [P, J // 16], U16)
+        second = sb("second", [P, J // 16], U16)
+        entry = sb("entry", [P, J // 16], U16)
+        x_rows = [sb("x_rows%d" % t, [P, T], F32) for t in range(PACK)]
+        tb_pair = sb("tb_pair", [P, 2, V], F32)
+        tb_rows = [tb_pair[:, t, :] for t in range(2)] + [sb("tb_rows%d" % t, [P, V], F32)[:] for t in range(2, PACK)]
+        so_rows = sb("so_rows", [P, PACK, J], F32)
+        fk_sb = sb("fk_sb", [P, PACK], F32)
+        fl_sb = sb("fl_sb", [P, PACK], F32)
+        w_raw = sb("w_raw", [P, 2 * R], U8)
+        w2_raw = sb("w2_raw", [P, R], U32)
+        wb_codes = sb("wb_codes", [P, N], U32)
+        raw_scales = sb("raw_scales", [P, 2 * R], U8)
+        planes = sb("planes", [P, 2 * R], U8)
+        wb_plane = sb("wb_plane", [P, N], U8)
+        rs_sb = sb("rs_sb", [P, HALVES, N], F32)
+        so_scaled = sb("so_scaled", [P, PACK, PAD + J], F32)
+
+        zeros = sb("zeros", [P, PACK, PAD], F32)
+        nc.gpsimd.memset(zeros[:], 0.0)
+        nc.scalar.activation(so_scaled[:, :, 0:PAD], zeros[:], ACT.Copy)
+        nc.vector.memset(raw_scales[:].bitcast(I32), 0)
+        nc.gpsimd.memset(wb_plane[:].bitcast(I32), 0)
+        nc.gpsimd.dma_start(fl_sb[:], fl.rearrange("(p t) o -> p (t o)", t=PACK))
+        nc.gpsimd.dma_start(fk_sb[:], fk.rearrange("(p t) o -> p (t o)", t=PACK))
+
+        x_view = xf.rearrange("(p t) n -> p t n", t=PACK)
+        tb_view = tb.rearrange("(p t) n -> p t n", t=PACK)
+        dma = nc.sync.dma_start
+        dma(second[:], offs2)
+        dma(x_rows[0][:], x_view[:, 0, :])
+        dma(raw_scales[0:16, 0:R].bitcast(I32), w_scales[0].bitcast(I32))
+        dma(raw_scales[0:16, R : 2 * R].bitcast(I32), w2_scales[0].bitcast(I32))
+        dma(first[:], offs)
+        for t in range(1, PACK):
+            dma(x_rows[t][:], x_view[:, t, :])
+        dma(so_rows[:], so.rearrange("(p t) n -> p t n", t=PACK))
+        dma(w_raw[:].bitcast(I32), w_words[0].bitcast(I32))
+        dma(w2_raw[:].bitcast(I32), w2_words[0].rearrange("p n t -> p (n t)").bitcast(I32))
+        nc.vector.tensor_copy(
+            planes[:, 0 : 2 * R].rearrange("p (s t m) -> p s t m", s=2, t=PACK),
+            raw_scales[:].rearrange("p (s m t) -> p s t m", s=2, t=PACK),
+        )
+        for q in range(1, 4):
+            dma(planes[32 * q : 32 * q + 4, :].bitcast(I32), planes[4 * q : 4 * q + 4, :].bitcast(I32))
+        dma(tb_pair[:], tb_view[:, 0:2, :])
+        dma(entry[:], offs3)
+        for t in range(2, PACK):
+            dma(tb_rows[t], tb_view[:, t, :])
+        dma(wb_codes[:].bitcast(I32), wb_words[0].rearrange("p n t -> p (n t)").bitcast(I32))
+        for q in range(4):
+            dma(wb_plane[32 * q : 32 * q + 4, :].bitcast(I32), wb_scales[0, 4 * q : 4 * q + 4, :].bitcast(I32))
+        dma(rs_sb[:], rs.rearrange("(h p) n -> p h n", p=P))
+
+        taken = sb("taken", [P, PACK, J], F32)
+        gaps = sb("gaps", [P, PACK, J], F32)
+        for t in range(PACK):
+            nc.scalar.activation(taken[:, t, :], x_rows[t][:].indirect(second[:]), ACT.Copy)
+            nc.vector.tensor_tensor(gaps[:, t, :], x_rows[t][:].indirect(first[:]), taken[:, t, :], ALU.subtract)
+        for t in range(PACK):
+            nc.scalar.activation(so_scaled[:, t, PAD:], so_rows[:, t, :], ACT.Copy, scale=fl_sb[:, t : t + 1])
+
+        w_codes = sb("w_codes", [P, 2 * R], U8)
+        w2_codes = sb("w2_codes", [P, R], U32)
+        nc.scalar.copy(
+            w_codes[:].bitcast(U16).rearrange("p (t m) -> p t m", t=PACK),
+            w_raw[:].bitcast(U16).rearrange("p (m t) -> p t m", t=PACK),
+        )
+
+        def woven(tile):
+            return tile[:].rearrange("p (c i t) -> p c t i", i=4, t=PACK)
+
+        def by_rows(ap):
+            return ap.rearrange("p t (c i) -> p c t i", i=4)
+
+        def quantised(name, values, fmt):
+            words = values.shape[1] // PACK
+            codes = sb(name + "_codes", [P, words], U32)
+            scales = sb(name + "_scales", [P, words], U8)
+            nc.vector.quantize_mx(out=codes[:].bitcast(fmt), scales=scales[:], in_=values)
+            return codes, scales
+
+        fk_wide = fk_sb[:].unsqueeze(1).unsqueeze(3).to_broadcast([P, J // 4, PACK, 4])
+        u_bf = keep.tile([P, PACK * J], BF16, name="u_bf", tag="rounded", align_bytes=64)
+        acc = [psum.tile([P, PACK, HALF], F32, name="acc%d" % h) for h in range(HALVES)]
+        nc.vector.tensor_tensor(woven(u_bf), by_rows(gaps[:]), fk_wide, ALU.mult)
+        nc.vector.tensor_copy(
+            w2_codes[:].bitcast(I32).rearrange("p (t m) -> p t m", t=PACK),
+            w2_raw[:].bitcast(I32).rearrange("p (m t) -> p t m", t=PACK),
+        )
+        u_codes, u_scales = quantised("u", u_bf[:], E4M3)
+        for h in range(HALVES):
+            for t in range(PACK):
+                nc.tensor.matmul_mx(
+                    acc[h][:, t, :],
+                    lhsT=w_codes[:, 2 * P * t : 2 * P * (t + 1)].bitcast(E2M1),
+                    lhsT_scale=planes[:, P * t : P * (t + 1)],
+                    rhs=u_codes[:, h * HALF : (h + 1) * HALF].bitcast(E4M3),
+                    rhs_scale=u_scales[:, h * HALF : (h + 1) * HALF],
+                    start=(t == 0),
+                    stop=False,
+                )
+        u2_whole = keep.tile([P, PACK * J], BF16, name="u2_whole", tag="rounded", align_bytes=64)
+        u2_bf = [u2_whole[:, h * PACK * HALF : (h + 1) * PACK * HALF] for h in range(HALVES)]
+        for h in range(HALVES):
+            j0 = PAD + h * HALF
+            nc.vector.scalar_tensor_tensor(
+                u2_bf[h].rearrange("p (j t) -> p j t", t=PACK),
+                so_scaled[:, :, j0 - 1 : j0 - 1 + HALF].rearrange("p t j -> p j t"),
+                -0.8,
+                so_scaled[:, :, j0 : j0 + HALF].rearrange("p t j -> p j t"),
+                ALU.mult,
+                ALU.add,
+            )
+        for h in range(HALVES):
+            u2_codes, u2_scales = quantised("u2_%d" % h, u2_bf[h], E5M2)
+            for t in range(PACK):
+                nc.tensor.matmul_mx(
+                    acc[h][:, t, :],
+                    lhsT=w2_codes[:, P * t : P * (t + 1)].bitcast(E5M2),
+                    lhsT_scale=planes[:, R + P * t : R + P * (t + 1)],
+                    rhs=u2_codes[:].bitcast(E5M2),
+                    rhs_scale=u2_scales[:],
+                    start=False,
+                    stop=(t == PACK - 1),
+                )
+
+        picked = [sb("picked%d" % h, [P, PACK, HALF], F32) for h in range(HALVES)]
+        for t in range(PACK):
+            for h in range(HALVES):
+                cols = entry[:, h * LIST_COLS : (h + 1) * LIST_COLS]
+                nc.scalar.activation(picked[h][:, t, :], tb_rows[t].indirect(cols), ACT.Copy)
+
+        residual = sb("residual", [P, HALVES, N], F32)
+        nc.gpsimd.tensor_scalar(residual[:], rs_sb[:], 0.3, 0.0, ALU.mult, ALU.add)
+
+        for h in range(HALVES):
+            over = sb("over%d" % h, [P, PACK, HALF], F32)
+            hid_bf = sb("hid_bf%d" % h, [P, PACK * HALF], BF16)
+            nc.vector.tensor_tensor(over[:], acc[h][:], picked[h][:], ALU.subtract)
+            nc.scalar.activation(woven(hid_bf), by_rows(over[:]), ACT.Relu)
+            hid_codes, hid_scales = quantised("hid%d" % h, hid_bf[:], E5M2)
+            prod = psum.tile([P, N], F32, name="prod%d" % h)
+            nc.tensor.matmul_mx(
+                prod[:],
+                lhsT=hid_codes[:].bitcast(E5M2),
+                lhsT_scale=hid_scales[:],
+                rhs=wb_codes[:].bitcast(E5M2),
+                rhs_scale=wb_plane[:],
+                start=True,
+                stop=True,
+            )
+            size = sb("size%d" % h, [P, N], F32)
+            peak = sb("peak%d" % h, [P, 1], F32)
+            inverse = sb("inverse%d" % h, [P, 1], F32)
+            result = sb("result%d" % h, [P, N], F32)
+            nc.scalar.activation(size[:], prod[:], ACT.Abs)
+            nc.vector.tensor_scalar(size[:], size[:], 0.2, None, ALU.add, ALU.max, accum_out=peak[:])
+            nc.vector.reciprocal(inverse[:], peak[:])
+            nc.vector.scalar_tensor_tensor(result[:], prod[:], inverse[:], residual[:, h, :], ALU.mult, ALU.add)
+            dma(out[h * HALF : (h + 1) * HALF, :], result[:])

@@ -40,8 +40,7 @@ def tile_list_sum_pickgaps_stepped_overtable_rowpeaks_kernel(
         second = sb("second", [P, J // 16], U16)
         entry = sb("entry", [P, J // 16], U16)
         x_rows = [sb("x_rows%d" % t, [P, T], F32) for t in range(PACK)]
-        tb_pair = sb("tb_pair", [P, 2, V], F32)
-        tb_rows = [tb_pair[:, t, :] for t in range(2)] + [sb("tb_rows%d" % t, [P, V], F32)[:] for t in range(2, PACK)]
+        tb_pairs = [sb("tb_pair%d" % g, [P, 2, V], F32) for g in range(2)]
         so_rows = sb("so_rows", [P, PACK, J], F32)
         fk_sb = sb("fk_sb", [P, PACK], F32)
         fl_sb = sb("fl_sb", [P, PACK], F32)
@@ -81,14 +80,13 @@ def tile_list_sum_pickgaps_stepped_overtable_rowpeaks_kernel(
         )
         for q in range(1, 4):
             dma(planes[32 * q : 32 * q + 4, :].bitcast(I32), planes[4 * q : 4 * q + 4, :].bitcast(I32))
-        dma(tb_pair[:], tb_view[:, 0:2, :])
+        dma(tb_pairs[0][:], tb_view[:, 0:2, :])
         dma(entry[:], offs3)
-        for t in range(2, PACK):
-            dma(tb_rows[t], tb_view[:, t, :])
+        dma(tb_pairs[1][:], tb_view[:, 2:4, :])
         dma(wb_codes[:].bitcast(I32), wb_words[0].rearrange("p n t -> p (n t)").bitcast(I32))
+        dma(rs_sb[:], rs.rearrange("(h p) n -> p h n", p=P))
         for q in range(4):
             dma(wb_plane[32 * q : 32 * q + 4, :].bitcast(I32), wb_scales[0, 4 * q : 4 * q + 4, :].bitcast(I32))
-        dma(rs_sb[:], rs.rearrange("(h p) n -> p h n", p=P))
 
         taken = sb("taken", [P, PACK, J], F32)
         gaps = sb("gaps", [P, PACK, J], F32)
@@ -103,6 +101,10 @@ def tile_list_sum_pickgaps_stepped_overtable_rowpeaks_kernel(
         nc.scalar.copy(
             w_codes[:].bitcast(U16).rearrange("p (t m) -> p t m", t=PACK),
             w_raw[:].bitcast(U16).rearrange("p (m t) -> p t m", t=PACK),
+        )
+        nc.scalar.copy(
+            w2_codes[:].rearrange("p (t c i) -> p c t i", t=PACK, i=4),
+            w2_raw[:].rearrange("p (c i t) -> p c t i", t=PACK, i=4),
         )
 
         def woven(tile):
@@ -119,13 +121,37 @@ def tile_list_sum_pickgaps_stepped_overtable_rowpeaks_kernel(
             return codes, scales
 
         fk_wide = fk_sb[:].unsqueeze(1).unsqueeze(3).to_broadcast([P, J // 4, PACK, 4])
-        u_bf = keep.tile([P, PACK * J], BF16, name="u_bf", tag="rounded", align_bytes=64)
+        u_bf = sb("u_bf", [P, PACK * J], BF16)
+        steps = [sb("steps%d" % h, [P, PACK, HALF], F32) for h in range(HALVES)]
+        u2_bf = [sb("u2_bf%d" % h, [P, PACK * HALF], BF16) for h in range(HALVES)]
         acc = [psum.tile([P, PACK, HALF], F32, name="acc%d" % h) for h in range(HALVES)]
+
+        def step(h):
+            j0 = PAD + h * HALF
+            nc.vector.scalar_tensor_tensor(
+                steps[h][:],
+                so_scaled[:, :, j0 - 1 : j0 - 1 + HALF],
+                -0.8,
+                so_scaled[:, :, j0 : j0 + HALF],
+                ALU.mult,
+                ALU.add,
+            )
+
+        def second_stream(h):
+            u2_codes, u2_scales = quantised("u2_%d" % h, u2_bf[h][:], E5M2)
+            for t in range(PACK):
+                nc.tensor.matmul_mx(
+                    acc[h][:, t, :],
+                    lhsT=w2_codes[:, P * t : P * (t + 1)].bitcast(E5M2),
+                    lhsT_scale=planes[:, R + P * t : R + P * (t + 1)],
+                    rhs=u2_codes[:].bitcast(E5M2),
+                    rhs_scale=u2_scales[:],
+                    start=False,
+                    stop=(t == PACK - 1),
+                )
+
         nc.vector.tensor_tensor(woven(u_bf), by_rows(gaps[:]), fk_wide, ALU.mult)
-        nc.vector.tensor_copy(
-            w2_codes[:].bitcast(I32).rearrange("p (t m) -> p t m", t=PACK),
-            w2_raw[:].bitcast(I32).rearrange("p (m t) -> p t m", t=PACK),
-        )
+        step(0)
         u_codes, u_scales = quantised("u", u_bf[:], E4M3)
         for h in range(HALVES):
             for t in range(PACK):
@@ -138,36 +164,18 @@ def tile_list_sum_pickgaps_stepped_overtable_rowpeaks_kernel(
                     start=(t == 0),
                     stop=False,
                 )
-        u2_whole = keep.tile([P, PACK * J], BF16, name="u2_whole", tag="rounded", align_bytes=64)
-        u2_bf = [u2_whole[:, h * PACK * HALF : (h + 1) * PACK * HALF] for h in range(HALVES)]
-        for h in range(HALVES):
-            j0 = PAD + h * HALF
-            nc.vector.scalar_tensor_tensor(
-                u2_bf[h].rearrange("p (j t) -> p j t", t=PACK),
-                so_scaled[:, :, j0 - 1 : j0 - 1 + HALF].rearrange("p t j -> p j t"),
-                -0.8,
-                so_scaled[:, :, j0 : j0 + HALF].rearrange("p t j -> p j t"),
-                ALU.mult,
-                ALU.add,
-            )
-        for h in range(HALVES):
-            u2_codes, u2_scales = quantised("u2_%d" % h, u2_bf[h], E5M2)
-            for t in range(PACK):
-                nc.tensor.matmul_mx(
-                    acc[h][:, t, :],
-                    lhsT=w2_codes[:, P * t : P * (t + 1)].bitcast(E5M2),
-                    lhsT_scale=planes[:, R + P * t : R + P * (t + 1)],
-                    rhs=u2_codes[:].bitcast(E5M2),
-                    rhs_scale=u2_scales[:],
-                    start=False,
-                    stop=(t == PACK - 1),
-                )
+        nc.vector.tensor_copy(woven(u2_bf[0]), by_rows(steps[0][:]))
+        step(1)
+        second_stream(0)
+        nc.vector.tensor_copy(woven(u2_bf[1]), by_rows(steps[1][:]))
+        second_stream(1)
 
         picked = [sb("picked%d" % h, [P, PACK, HALF], F32) for h in range(HALVES)]
-        for t in range(PACK):
+        for g in range(2):
             for h in range(HALVES):
-                cols = entry[:, h * LIST_COLS : (h + 1) * LIST_COLS]
-                nc.scalar.activation(picked[h][:, t, :], tb_rows[t].indirect(cols), ACT.Copy)
+                for e in range(2):
+                    cols = entry[:, h * LIST_COLS : (h + 1) * LIST_COLS]
+                    nc.scalar.activation(picked[h][:, 2 * g + e, :], tb_pairs[g][:, e, :].indirect(cols), ACT.Copy)
 
         residual = sb("residual", [P, HALVES, N], F32)
         nc.gpsimd.tensor_scalar(residual[:], rs_sb[:], 0.3, 0.0, ALU.mult, ALU.add)

@@ -23,6 +23,7 @@ HALF = 128
 HALVES = J // HALF
 LIST_COLS = HALF // 16
 PAD = 4
+RUN = 2
 
 
 def tile_list_sum_pickgaps_stepped_overtable_rowpeaks_kernel(
@@ -91,8 +92,13 @@ def tile_list_sum_pickgaps_stepped_overtable_rowpeaks_kernel(
         taken = sb("taken", [P, PACK, J], F32)
         gaps = sb("gaps", [P, PACK, J], F32)
         for t in range(PACK):
-            nc.scalar.activation(taken[:, t, :], x_rows[t][:].indirect(second[:]), ACT.Copy)
-            nc.vector.tensor_tensor(gaps[:, t, :], x_rows[t][:].indirect(first[:]), taken[:, t, :], ALU.subtract)
+            pieces = [(0, J)] if t < PACK - 1 else [(h * HALF, (h + 1) * HALF) for h in range(HALVES)]
+            for j0, j1 in pieces:
+                cols = slice(j0 // 16, j1 // 16)
+                nc.scalar.activation(taken[:, t, j0:j1], x_rows[t][:].indirect(second[:, cols]), ACT.Copy)
+                nc.vector.tensor_tensor(
+                    gaps[:, t, j0:j1], x_rows[t][:].indirect(first[:, cols]), taken[:, t, j0:j1], ALU.subtract
+                )
         for t in range(PACK):
             nc.scalar.activation(so_scaled[:, t, PAD:], so_rows[:, t, :], ACT.Copy, scale=fl_sb[:, t : t + 1])
 
@@ -108,10 +114,10 @@ def tile_list_sum_pickgaps_stepped_overtable_rowpeaks_kernel(
         )
 
         def woven(tile):
-            return tile[:].rearrange("p (c i t) -> p c t i", i=4, t=PACK)
+            return tile.rearrange("p (c i t) -> p c t i", i=RUN, t=PACK)
 
         def by_rows(ap):
-            return ap.rearrange("p t (c i) -> p c t i", i=4)
+            return ap.rearrange("p t (c i) -> p c t i", i=RUN)
 
         def quantised(name, values, fmt):
             words = values.shape[1] // PACK
@@ -120,8 +126,8 @@ def tile_list_sum_pickgaps_stepped_overtable_rowpeaks_kernel(
             nc.vector.quantize_mx(out=codes[:].bitcast(fmt), scales=scales[:], in_=values)
             return codes, scales
 
-        fk_wide = fk_sb[:].unsqueeze(1).unsqueeze(3).to_broadcast([P, J // 4, PACK, 4])
-        u_bf = sb("u_bf", [P, PACK * J], BF16)
+        fk_wide = fk_sb[:].unsqueeze(1).unsqueeze(3).to_broadcast([P, HALF // RUN, PACK, RUN])
+        u_bf = [sb("u_bf%d" % h, [P, PACK * HALF], BF16) for h in range(HALVES)]
         steps = [sb("steps%d" % h, [P, PACK, HALF], F32) for h in range(HALVES)]
         u2_bf = [sb("u2_bf%d" % h, [P, PACK * HALF], BF16) for h in range(HALVES)]
         acc = [psum.tile([P, PACK, HALF], F32, name="acc%d" % h) for h in range(HALVES)]
@@ -150,24 +156,28 @@ def tile_list_sum_pickgaps_stepped_overtable_rowpeaks_kernel(
                     stop=(t == PACK - 1),
                 )
 
-        nc.vector.tensor_tensor(woven(u_bf), by_rows(gaps[:]), fk_wide, ALU.mult)
-        step(0)
-        u_codes, u_scales = quantised("u", u_bf[:], E4M3)
-        for h in range(HALVES):
+        def first_stream(h):
+            u_codes, u_scales = quantised("u_%d" % h, u_bf[h][:], E4M3)
             for t in range(PACK):
                 nc.tensor.matmul_mx(
                     acc[h][:, t, :],
                     lhsT=w_codes[:, 2 * P * t : 2 * P * (t + 1)].bitcast(E2M1),
                     lhsT_scale=planes[:, P * t : P * (t + 1)],
-                    rhs=u_codes[:, h * HALF : (h + 1) * HALF].bitcast(E4M3),
-                    rhs_scale=u_scales[:, h * HALF : (h + 1) * HALF],
+                    rhs=u_codes[:].bitcast(E4M3),
+                    rhs_scale=u_scales[:],
                     start=(t == 0),
                     stop=False,
                 )
-        nc.vector.tensor_copy(woven(u2_bf[0]), by_rows(steps[0][:]))
+
+        for h in range(HALVES):
+            nc.vector.tensor_tensor(woven(u_bf[h][:]), by_rows(gaps[:, :, h * HALF : (h + 1) * HALF]), fk_wide, ALU.mult)
+        first_stream(0)
+        step(0)
+        first_stream(1)
+        nc.vector.tensor_copy(woven(u2_bf[0][:]), by_rows(steps[0][:]))
         step(1)
         second_stream(0)
-        nc.vector.tensor_copy(woven(u2_bf[1]), by_rows(steps[1][:]))
+        nc.vector.tensor_copy(woven(u2_bf[1][:]), by_rows(steps[1][:]))
         second_stream(1)
 
         picked = [sb("picked%d" % h, [P, PACK, HALF], F32) for h in range(HALVES)]
@@ -184,7 +194,10 @@ def tile_list_sum_pickgaps_stepped_overtable_rowpeaks_kernel(
             over = sb("over%d" % h, [P, PACK, HALF], F32)
             hid_bf = sb("hid_bf%d" % h, [P, PACK * HALF], BF16)
             nc.vector.tensor_tensor(over[:], acc[h][:], picked[h][:], ALU.subtract)
-            nc.scalar.activation(woven(hid_bf), by_rows(over[:]), ACT.Relu)
+            if h < HALVES - 1:
+                nc.scalar.activation(woven(hid_bf[:]), by_rows(over[:]), ACT.Relu)
+            else:
+                nc.vector.tensor_scalar_max(woven(hid_bf[:]), by_rows(over[:]), 0.0)
             hid_codes, hid_scales = quantised("hid%d" % h, hid_bf[:], E5M2)
             prod = psum.tile([P, N], F32, name="prod%d" % h)
             nc.tensor.matmul_mx(

from contextlib import ExitStack

import concourse.mybir as mybir

K, T, J, R, F, V, N = 512, 512, 256, 512, 512, 512, 256
FLOPS = 2 * (K * R * J + F * R * J + R * J * N)

F32 = mybir.dt.float32
BF16 = mybir.dt.bfloat16
I32 = mybir.dt.int32
U32 = mybir.dt.uint32
U16 = mybir.dt.uint16
U8 = mybir.dt.uint8
E4M3 = mybir.dt.float8_e4m3fn_x4
E5M2 = mybir.dt.float8_e5m2_x4
E2M1 = mybir.dt.float4_e2m1fn_x4
ALU = mybir.AluOpType
ACT = mybir.ActivationFunctionType

P = 128
PACK = 4
HALF = 128
HALVES = J // HALF
LIST_COLS = HALF // 16
PAD = 4
RUN = 2


def tile_list_sum_pickgaps_stepped_overtable_rowpeaks_kernel(
    tc, xf, fk, w_words, w_scales, so, fl, w2_words, w2_scales, tb, wb_words, wb_scales, rs, offs, offs2, offs3, out
):
    nc = tc.nc
    with ExitStack() as ctx:
        keep = ctx.enter_context(tc.tile_pool(name="keep", bufs=1))
        psum = ctx.enter_context(tc.psum_pool(name="psum", bufs=1))

        def sb(name, shape, dtype):
            return keep.tile(shape, dtype, name=name, align_bytes=64)

        first = sb("first", [P, J // 16], U16)
        second = sb("second", [P, J // 16], U16)
        entry = sb("entry", [P, J // 16], U16)
        x_rows = [sb("x_rows%d" % t, [P, T], F32) for t in range(PACK)]
        tb_pairs = [sb("tb_pair%d" % g, [P, 2, V], F32) for g in range(2)]
        so_rows = sb("so_rows", [P, PACK, J], F32)
        fk_sb = sb("fk_sb", [P, PACK], F32)
        fl_sb = sb("fl_sb", [P, PACK], F32)
        w_raw = sb("w_raw", [P, 2 * R], U8)
        w2_raw = sb("w2_raw", [P, R], U32)
        wb_codes = sb("wb_codes", [P, N], U32)
        raw_scales = sb("raw_scales", [P, 2 * R], U8)
        planes = sb("planes", [P, 2 * R], U8)
        wb_plane = sb("wb_plane", [P, N], U8)
        rs_sb = sb("rs_sb", [P, HALVES, N], F32)
        so_scaled = sb("so_scaled", [P, PACK, PAD + J], F32)

        zeros = sb("zeros", [P, PACK, PAD], F32)
        nc.gpsimd.memset(zeros[:], 0.0)
        nc.scalar.activation(so_scaled[:, :, 0:PAD], zeros[:], ACT.Copy)
        nc.vector.memset(raw_scales[:].bitcast(I32), 0)
        nc.gpsimd.memset(wb_plane[:].bitcast(I32), 0)
        nc.gpsimd.dma_start(fl_sb[:], fl.rearrange("(p t) o -> p (t o)", t=PACK))
        nc.gpsimd.dma_start(fk_sb[:], fk.rearrange("(p t) o -> p (t o)", t=PACK))

        x_view = xf.rearrange("(p t) n -> p t n", t=PACK)
        tb_view = tb.rearrange("(p t) n -> p t n", t=PACK)
        dma = nc.sync.dma_start
        dma(second[:], offs2)
        dma(x_rows[0][:], x_view[:, 0, :])
        dma(raw_scales[0:16, 0:R].bitcast(I32), w_scales[0].bitcast(I32))
        dma(raw_scales[0:16, R : 2 * R].bitcast(I32), w2_scales[0].bitcast(I32))
        dma(first[:], offs)
        for t in range(1, PACK):
            dma(x_rows[t][:], x_view[:, t, :])
        dma(so_rows[:], so.rearrange("(p t) n -> p t n", t=PACK))
        dma(w_raw[:].bitcast(I32), w_words[0].bitcast(I32))
        dma(w2_raw[:].bitcast(I32), w2_words[0].rearrange("p n t -> p (n t)").bitcast(I32))
        nc.vector.tensor_copy(
            planes[:, 0 : 2 * R].rearrange("p (s t m) -> p s t m", s=2, t=PACK),
            raw_scales[:].rearrange("p (s m t) -> p s t m", s=2, t=PACK),
        )
        for q in range(1, 4):
            dma(planes[32 * q : 32 * q + 4, :].bitcast(I32), planes[4 * q : 4 * q + 4, :].bitcast(I32))
        dma(tb_pairs[0][:], tb_view[:, 0:2, :])
        dma(entry[:], offs3)
        dma(tb_pairs[1][:], tb_view[:, 2:4, :])
        dma(wb_codes[:].bitcast(I32), wb_words[0].rearrange("p n t -> p (n t)").bitcast(I32))
        dma(rs_sb[:], rs.rearrange("(h p) n -> p h n", p=P))
        for q in range(4):
            dma(wb_plane[32 * q : 32 * q + 4, :].bitcast(I32), wb_scales[0, 4 * q : 4 * q + 4, :].bitcast(I32))

        taken = sb("taken", [P, PACK, J], F32)
        gaps = sb("gaps", [P, PACK, J], F32)
        for t in range(PACK):
            pieces = [(0, J)] if t < PACK - 1 else [(h * HALF, (h + 1) * HALF) for h in range(HALVES)]
            for j0, j1 in pieces:
                cols = slice(j0 // 16, j1 // 16)
                nc.scalar.activation(taken[:, t, j0:j1], x_rows[t][:].indirect(second[:, cols]), ACT.Copy)
                nc.vector.tensor_tensor(
                    gaps[:, t, j0:j1], x_rows[t][:].indirect(first[:, cols]), taken[:, t, j0:j1], ALU.subtract
                )
        for t in range(PACK):
            nc.scalar.activation(so_scaled[:, t, PAD:], so_rows[:, t, :], ACT.Copy, scale=fl_sb[:, t : t + 1])

        w_codes = sb("w_codes", [P, 2 * R], U8)
        w2_codes = sb("w2_codes", [P, R], U32)
        nc.scalar.copy(
            w_codes[:].bitcast(U16).rearrange("p (t m) -> p t m", t=PACK),
            w_raw[:].bitcast(U16).rearrange("p (m t) -> p t m", t=PACK),
        )
        nc.scalar.copy(
            w2_codes[:].rearrange("p (t c i) -> p c t i", t=PACK, i=4),
            w2_raw[:].rearrange("p (c i t) -> p c t i", t=PACK, i=4),
        )

        def woven(tile):
            return tile.rearrange("p (c i t) -> p c t i", i=RUN, t=PACK)

        def by_rows(ap):
            return ap.rearrange("p t (c i) -> p c t i", i=RUN)

        def quantised(name, values, fmt):
            words = values.shape[1] // PACK
            codes = sb(name + "_codes", [P, words], U32)
            scales = sb(name + "_scales", [P, words], U8)
            nc.vector.quantize_mx(out=codes[:].bitcast(fmt), scales=scales[:], in_=values)
            return codes, scales

        fk_wide = fk_sb[:].unsqueeze(1).unsqueeze(3).to_broadcast([P, HALF // RUN, PACK, RUN])
        u_bf = [sb("u_bf%d" % h, [P, PACK * HALF], BF16) for h in range(HALVES)]
        steps = [sb("steps%d" % h, [P, PACK, HALF], F32) for h in range(HALVES)]
        u2_bf = [sb("u2_bf%d" % h, [P, PACK * HALF], BF16) for h in range(HALVES)]
        acc = [psum.tile([P, PACK, HALF], F32, name="acc%d" % h) for h in range(HALVES)]

        def step(h):
            j0 = PAD + h * HALF
            nc.vector.scalar_tensor_tensor(
                steps[h][:],
                so_scaled[:, :, j0 - 1 : j0 - 1 + HALF],
                -0.8,
                so_scaled[:, :, j0 : j0 + HALF],
                ALU.mult,
                ALU.add,
            )

        def second_stream(h):
            u2_codes, u2_scales = quantised("u2_%d" % h, u2_bf[h][:], E5M2)
            for t in range(PACK):
                nc.tensor.matmul_mx(
                    acc[h][:, t, :],
                    lhsT=w2_codes[:, P * t : P * (t + 1)].bitcast(E5M2),
                    lhsT_scale=planes[:, R + P * t : R + P * (t + 1)],
                    rhs=u2_codes[:].bitcast(E5M2),
                    rhs_scale=u2_scales[:],
                    start=False,
                    stop=(t == PACK - 1),
                )

        def first_stream(h):
            u_codes, u_scales = quantised("u_%d" % h, u_bf[h][:], E4M3)
            for t in range(PACK):
                nc.tensor.matmul_mx(
                    acc[h][:, t, :],
                    lhsT=w_codes[:, 2 * P * t : 2 * P * (t + 1)].bitcast(E2M1),
                    lhsT_scale=planes[:, P * t : P * (t + 1)],
                    rhs=u_codes[:].bitcast(E4M3),
                    rhs_scale=u_scales[:],
                    start=(t == 0),
                    stop=False,
                )

        for h in range(HALVES):
            nc.vector.tensor_tensor(woven(u_bf[h][:]), by_rows(gaps[:, :, h * HALF : (h + 1) * HALF]), fk_wide, ALU.mult)
        first_stream(0)
        step(0)
        first_stream(1)
        nc.vector.tensor_copy(woven(u2_bf[0][:]), by_rows(steps[0][:]))
        step(1)
        second_stream(0)
        nc.vector.tensor_copy(woven(u2_bf[1][:]), by_rows(steps[1][:]))
        second_stream(1)

        picked = [sb("picked%d" % h, [P, PACK, HALF], F32) for h in range(HALVES)]
        for g in range(2):
            for h in range(HALVES):
                for e in range(2):
                    cols = entry[:, h * LIST_COLS : (h + 1) * LIST_COLS]
                    nc.scalar.activation(picked[h][:, 2 * g + e, :], tb_pairs[g][:, e, :].indirect(cols), ACT.Copy)

        residual = sb("residual", [P, HALVES, N], F32)
        nc.gpsimd.tensor_scalar(residual[:], rs_sb[:], 0.3, 0.0, ALU.mult, ALU.add)

        for h in range(HALVES):
            over = sb("over%d" % h, [P, PACK, HALF], F32)
            hid_bf = sb("hid_bf%d" % h, [P, PACK * HALF], BF16)
            nc.vector.tensor_tensor(over[:], acc[h][:], picked[h][:], ALU.subtract)
            if h < HALVES - 1:
                nc.scalar.activation(woven(hid_bf[:]), by_rows(over[:]), ACT.Relu)
            else:
                nc.vector.tensor_scalar_max(woven(hid_bf[:]), by_rows(over[:]), 0.0)
            hid_codes, hid_scales = quantised("hid%d" % h, hid_bf[:], E5M2)
            prod = psum.tile([P, N], F32, name="prod%d" % h)
            nc.tensor.matmul_mx(
                prod[:],
                lhsT=hid_codes[:].bitcast(E5M2),
                lhsT_scale=hid_scales[:],
                rhs=wb_codes[:].bitcast(E5M2),
                rhs_scale=wb_plane[:],
                start=True,
                stop=True,
            )
            size = sb("size%d" % h, [P, N], F32)
            peak = sb("peak%d" % h, [P, 1], F32)
            inverse = sb("inverse%d" % h, [P, 1], F32)
            result = sb("result%d" % h, [P, N], F32)
            nc.scalar.activation(size[:], prod[:], ACT.Abs)
            nc.vector.tensor_scalar(size[:], size[:], 0.2, None, ALU.add, ALU.max, accum_out=peak[:])
            nc.vector.reciprocal(inverse[:], peak[:])
            nc.vector.scalar_tensor_tensor(result[:], prod[:], inverse[:], residual[:, h, :], ALU.mult, ALU.add)
            dma(out[h * HALF : (h + 1) * HALF, :], result[:])
